import numpy as np
import ml_dtypes


def mxq(x, axis, fmt="e4m3"):
    dtype, down = {"e4m3": (ml_dtypes.float8_e4m3fn, 7), "e5m2": (ml_dtypes.float8_e5m2, 14)}[fmt]
    v = np.moveaxis(np.asarray(x, np.float32).astype(ml_dtypes.bfloat16).astype(np.float64), axis, -1)
    blocks = v.reshape(v.shape[:-1] + (-1, 32))
    amax = np.abs(blocks).max(-1, keepdims=True)
    byte = np.maximum(np.where(amax > 0, np.frexp(amax)[1] - 1 + 127, 0) - down, 1)
    scale = np.exp2(byte - 127.0)
    codes = (blocks / scale).astype(np.float32).astype(dtype).astype(np.float64)
    return np.moveaxis((codes * scale).reshape(v.shape), -1, axis)


WIDE = False


def mx_kscale(k):
    if not WIDE:
        return np.ones(k)
    levels = np.array([24, -24, 12, -12, 0])
    if k % 512:
        return np.exp2(np.random.permutation(np.resize(levels, k // 32))).repeat(32)
    a = np.empty((k // 512, 16))
    for p in range(k // 512):
        a[p, :8] = np.random.permutation(np.resize(levels, 8))
        for g in range(8):
            far = levels[np.abs(levels - a[p, g]) >= 10]
            a[p, g + 8] = far[np.random.randint(len(far))]
    return np.exp2(a.ravel()).repeat(32)


def f64(x):
    return np.asarray(x).astype(np.float64)


def striped(idx):
    return np.tile(idx.reshape(-1, 16).T, (8, 1)).astype(np.uint16)


def unstriped(offs):
    return offs[:16].T.reshape(-1).astype(np.int64)


E2M1 = np.array([0.0, 0.5, 1.0, 1.5, 2.0, 3.0, 4.0, 6.0, -0.0, -0.5, -1.0, -1.5, -2.0, -3.0, -4.0, -6.0])


def pack_weight(w, fmt):
    k, n = w.shape
    w = f64(np.asarray(w, np.float32).astype(ml_dtypes.bfloat16)).reshape(k // 32, 32, n)
    amax = np.abs(w).max(1)
    if fmt == "e4m3":
        byte = np.frexp(amax)[1] - 1 + 127 - 7
    else:
        mant, ex = np.frexp(amax / 6.0)
        byte = np.where(mant > 0.5, ex, ex - 1) + 127
    byte = np.clip(np.where(amax > 0, byte, 1), 1, 254)
    scaled = (w * np.exp2(127.0 - byte)[:, None, :]).reshape(k, n).astype(np.float32)
    by_word = np.ascontiguousarray(scaled.reshape(k // 512, 128, 4, n).transpose(0, 1, 3, 2))
    if fmt == "e4m3":
        words = by_word.astype(ml_dtypes.float8_e4m3fn).view(np.uint8)
    else:
        c = by_word.astype(ml_dtypes.float4_e2m1fn).view(np.uint8) & 0xF
        words = (c[..., 0::2] | (c[..., 1::2] << 4)).reshape(k // 512, 128, 2 * n)
    return np.ascontiguousarray(words), np.ascontiguousarray(byte.astype(np.uint8).reshape(k // 512, 16, n))


def unpack_weight(words, scales, fmt):
    g, _, n = scales.shape
    words = np.ascontiguousarray(words).reshape(g, 128, n, -1)
    if fmt == "e4m3":
        vals = words.view(ml_dtypes.float8_e4m3fn).astype(np.float64)
    else:
        nib = np.empty((g, 128, n, 4), np.uint8)
        nib[..., 0::2] = words & 0xF
        nib[..., 1::2] = words >> 4
        vals = E2M1[nib]
    vals = vals * np.repeat(np.exp2(scales.astype(np.float64) - 127.0), 8, axis=1)[..., None]
    return vals.transpose(0, 1, 3, 2).reshape(g * 512, n)


def pack_table4(v):
    words, scales = pack_weight(v, "e2m1")
    g, t = words.shape[0] // 2, v.shape[1]
    return np.ascontiguousarray(words.reshape(g, 2, 128, t, 2).transpose(0, 2, 3, 1, 4).reshape(g, 128, t, 4)), scales


def unpack_table4(words, scales):
    g, _, t, _ = words.shape
    return unpack_weight(words.reshape(g, 128, t, 2, 2).transpose(0, 3, 1, 2, 4).reshape(2 * g, 128, 2 * t), scales, "e2m1")


def sigm(f):
    return 1.0 / (1.0 + np.exp(-np.maximum(f, -700.0)))


def gelu(f):
    return 0.5 * f * (1.0 + np.tanh(np.sqrt(2.0 / np.pi) * (f + 0.044715 * f**3)))


K, N, T, J = 1024, 1024, 2048, 1024


def setup_inputs():
    n = np.random.standard_normal
    s = mx_kscale(K)[:, None]
    p_tab = pack_table4(n((K, T)) * s)
    p_wg = pack_weight(n((K, N)) / np.sqrt(K) / s, "e4m3")
    return {
        "tab_words": p_tab[0],
        "tab_scales": p_tab[1],
        "wg_words": p_wg[0],
        "wg_scales": p_wg[1],
        "wh": (n((K, N)) / np.sqrt(K) / s).astype(np.float32),
        "bg": (0.3 * n(N) - 1.0).astype(np.float32),
        "rT": (n((N, T))).astype(np.float32),
        "offs": striped(np.random.permutation(T)[:J]),
    }


def reference(tab_words, tab_scales, wg_words, wg_scales, wh, bg, rT, offs):
    idx = unstriped(offs)
    tab_ = unpack_table4(tab_words, tab_scales)[:, idx]
    wg_ = unpack_weight(wg_words, wg_scales, "e4m3")
    wh_ = mxq(f64(wh), 0, "e4m3")
    ga = wg_.T @ tab_
    gate = sigm(ga + f64(bg)[:, None])
    ha = wh_.T @ tab_
    return f64(rT)[:, idx] + gate * (gelu(ha) - f64(rT)[:, idx])

@@ -1,0 +1,184 @@
+from contextlib import ExitStack
+
+import concourse.mybir as mybir
+from concourse.masks import make_identity
+
+K, N, T, J = 1024, 1024, 2048, 1024
+FLOPS = 2 * 2 * K * N * J
+
+F32 = mybir.dt.float32
+BF16 = mybir.dt.bfloat16
+I32 = mybir.dt.int32
+U32 = mybir.dt.uint32
+U16 = mybir.dt.uint16
+U8 = mybir.dt.uint8
+FP8X4 = mybir.dt.float8_e4m3fn_x4
+FP4X4 = mybir.dt.float4_e2m1fn_x4
+ALU = mybir.AluOpType
+ACT = mybir.ActivationFunctionType
+
+P = 128
+PACK = 4
+PASSES = K // (P * PACK)
+HALF = 512
+HALVES = J // HALF
+TILES = N // P
+CHUNKS = (128, 128, 256, 512)
+WG_CHUNKS = (256, 768)
+
+
+def tile_list_hwayt_gelu_kernel(
+    tc, tab_words, tab_scales, wg_words, wg_scales, wh, bg, rT, offs, out
+):
+    nc = tc.nc
+    with ExitStack() as ctx:
+        keep = ctx.enter_context(tc.tile_pool(name="keep", bufs=1))
+        ring = ctx.enter_context(tc.tile_pool(name="ring", bufs=2))
+        psum = ctx.enter_context(tc.psum_pool(name="psum", bufs=4))
+
+        offsets = keep.tile([P, J // 16], U16, name="offsets")
+        nc.sync.dma_start(offsets[:], offs)
+
+        tab_w = keep.tile([P, T], I32, name="tab_w", align_bytes=64)
+        nc.sync.dma_start(tab_w[:], tab_words[0].rearrange("p t i -> p (t i)").bitcast(I32))
+
+        tab_s = keep.tile([P, T], U8, name="tab_s", align_bytes=64)
+        nc.vector.memset(tab_s[:].bitcast(I32), 0)
+        for q in range(4):
+            nc.scalar.dma_start(
+                tab_s[32 * q : 32 * q + 8, :].bitcast(I32),
+                tab_scales[:, 4 * q : 4 * q + 4, :].bitcast(I32),
+            )
+        zero_in = keep.tile([P, 1], F32, name="zero_in")
+        nc.vector.memset(zero_in[:], 0.0)
+        zero = keep.tile([P, 1], F32, name="zero")
+        nc.scalar.activation(zero[:], zero_in[:], ACT.Gelu_apprx_tanh, bias=zero_in[:])
+        wg_s = keep.tile([P, PASSES, N], U8, name="wg_s", align_bytes=64)
+        nc.vector.memset(wg_s[:].rearrange("p a t -> p (a t)").bitcast(I32), 0)
+        v_s = [keep.tile([P, J], U8, name="v_s%d" % a, align_bytes=64) for a in range(PASSES)]
+        nc.vector.memset(v_s[1][:].bitcast(I32), 0)
+
+        bg_rows = keep.tile([P, P], F32, name="bg_rows")
+        nc.gpsimd.memset(bg_rows[:], 0.0)
+        nc.gpsimd.dma_start(bg_rows[0:TILES, :], bg.rearrange("(c p) -> c p", p=P))
+        ident = keep.tile([P, P], F32, name="ident")
+        make_identity(nc, ident[:])
+
+        wg_starts = [sum(WG_CHUNKS[:c]) for c in range(len(WG_CHUNKS))]
+        starts = [sum(CHUNKS[:c]) for c in range(len(CHUNKS))]
+        wh_raw, wg_w, r = {}, {}, {}
+
+        def load_wh(c):
+            for a in range(PASSES):
+                wh_raw[c, a] = keep.tile([P, PACK, CHUNKS[c]], F32, name="wh_raw%d_%d" % (c, a))
+                rows = wh[512 * a : 512 * (a + 1), starts[c] : starts[c] + CHUNKS[c]]
+                nc.sync.dma_start(wh_raw[c, a][:], rows.rearrange("(p i) n -> p i n", i=PACK))
+
+        def load_wg(c):
+            wg_w[c] = keep.tile([P, PASSES, WG_CHUNKS[c]], I32, name="wg_w%d" % c, align_bytes=64)
+            words = wg_words.rearrange("a p n i -> p a (n i)")
+            nc.sync.dma_start(wg_w[c][:], words[:, :, 4 * wg_starts[c] : 4 * (wg_starts[c] + WG_CHUNKS[c])].bitcast(I32))
+
+        def load_r(i):
+            r[i] = keep.tile([P, T], F32, name="r%d" % i)
+            nc.sync.dma_start(r[i][:], rT[P * i : P * (i + 1), :])
+
+        load_wh(0)
+        for q in range(4):
+            nc.sync.dma_start(
+                wg_s[32 * q : 32 * q + 4, :, :].bitcast(I32),
+                wg_scales[:, 4 * q : 4 * q + 4, :].rearrange("a r n -> r a n").bitcast(I32),
+            )
+        load_r(0)
+        load_wg(0)
+        load_wh(1)
+        load_r(1)
+        load_wh(2)
+        load_r(2)
+        load_wg(1)
+        load_r(3)
+        load_wh(3)
+        for i in range(4, TILES):
+            load_r(i)
+
+        bg_t = psum.tile([P, P], F32, name="bg_t", tag="ga")
+        nc.tensor.transpose(bg_t[:], bg_rows[:], ident[:])
+        half_bg = keep.tile([P, TILES], F32, name="half_bg")
+        nc.scalar.activation(half_bg[:], bg_t[:, 0:TILES], ACT.Copy, scale=0.5)
+
+        nc.vector.tensor_copy(v_s[0][:], tab_s[:].indirect(offsets[:]))
+        nc.scalar.dma_start(v_s[1][0:100, :].bitcast(I32), v_s[0][4:104, :].bitcast(I32))
+        v_w = {}
+        for h in range(HALVES):
+            picks = offsets[:, h * (HALF // 16) : (h + 1) * (HALF // 16)]
+            pairs = keep.tile([P, HALF], U32, name="pairs%d" % h, align_bytes=64)
+            nc.vector.tensor_copy(pairs[:], tab_w[:].bitcast(U32).indirect(picks))
+            v_w[h] = keep.tile([P, PASSES, HALF], U16, name="v_w%d" % h, align_bytes=64)
+            nc.vector.tensor_copy(v_w[h][:], pairs[:].bitcast(U16).rearrange("p (j a) -> p a j", a=PASSES))
+
+        wh_w, wh_s = {}, {}
+
+        def quantize_wh(c):
+            for a in range(PASSES):
+                grouped = ring.tile([P, CHUNKS[c], PACK], BF16, name="grouped", tag="grouped", align_bytes=64)
+                nc.scalar.copy(
+                    grouped[:].rearrange("p (c n) i -> p c i n", n=4),
+                    wh_raw[c, a][:].rearrange("p i (c n) -> p c i n", n=4),
+                )
+                wh_w[c, a] = keep.tile([P, CHUNKS[c]], U32, name="wh_w%d_%d" % (c, a), align_bytes=64)
+                wh_s[c, a] = keep.tile([P, CHUNKS[c]], U8, name="wh_s%d_%d" % (c, a), align_bytes=64)
+                nc.vector.quantize_mx(
+                    out=wh_w[c, a][:].bitcast(FP8X4),
+                    scales=wh_s[c, a][:],
+                    in_=grouped[:].rearrange("p n i -> p (n i)"),
+                )
+
+        def product(bank, h, words, scales):
+            for a in range(PASSES):
+                nc.tensor.matmul_mx(
+                    out=bank[:],
+                    lhsT=words[a].bitcast(FP8X4),
+                    lhsT_scale=scales[a],
+                    rhs=v_w[h][:, a, :].bitcast(FP4X4),
+                    rhs_scale=v_s[a][:, h * HALF : (h + 1) * HALF],
+                    start=(a == 0),
+                    stop=(a == PASSES - 1),
+                )
+
+        for i in range(TILES):
+            c = max(x for x in range(len(CHUNKS)) if starts[x] <= P * i)
+            if starts[c] == P * i:
+                quantize_wh(c)
+            cols = slice(P * i - starts[c], P * (i + 1) - starts[c])
+            g = max(x for x in range(len(WG_CHUNKS)) if wg_starts[x] <= P * i)
+            gcols = slice(P * i - wg_starts[g], P * (i + 1) - wg_starts[g])
+            made = keep.tile([P, J], F32, name="made%d" % i)
+            th = keep.tile([P, J], F32, name="th%d" % i)
+            for h in range(HALVES):
+                js = slice(h * HALF, (h + 1) * HALF)
+                ha = psum.tile([P, HALF], F32, name="ha", tag="ha")
+                product(ha, h, [wh_w[c, a][:, cols] for a in range(PASSES)], [wh_s[c, a][:, cols] for a in range(PASSES)])
+                nc.scalar.activation(made[:, js], ha[:], ACT.Gelu_apprx_tanh, bias=zero[:])
+            for h in range(HALVES):
+                js = slice(h * HALF, (h + 1) * HALF)
+                ga = psum.tile([P, HALF], F32, name="ga", tag="ga")
+                product(ga, h, [wg_w[g][:, a, gcols] for a in range(PASSES)], [wg_s[:, a, P * i : P * (i + 1)] for a in range(PASSES)])
+                nc.scalar.activation(th[:, js], ga[:], ACT.Tanh, bias=half_bg[:, i : i + 1], scale=0.5)
+            diff = {}
+            for h in range(HALVES):
+                js = slice(h * HALF, (h + 1) * HALF)
+                picks = offsets[:, h * (HALF // 16) : (h + 1) * (HALF // 16)]
+                diff[h] = ring.tile([P, HALF], F32, name="diff%d" % h, tag="diff%d" % h)
+                nc.vector.tensor_tensor(diff[h][:], r[i][:].indirect(picks), made[:, js], ALU.subtract)
+            for h in range(HALVES):
+                js = slice(h * HALF, (h + 1) * HALF)
+                nc.vector.scalar_tensor_tensor(th[:, js], th[:, js], 1.0, diff[h][:], ALU.subtract, ALU.mult)
+            for h in range(HALVES):
+                js = slice(h * HALF, (h + 1) * HALF)
+                nc.vector.scalar_tensor_tensor(made[:, js], th[:, js], -0.5, made[:, js], ALU.mult, ALU.add)
+            if i < TILES - 1:
+                nc.sync.dma_start(out[P * i : P * (i + 1), :], made[:])
+            else:
+                for h in range(HALVES):
+                    js = slice(h * HALF, (h + 1) * HALF)
+                    nc.sync.dma_start(out[P * i : P * (i + 1), js], made[:, js])

@@ -23,7 +23,7 @@ PASSES = K // (P * PACK)
 HALF = 512
 HALVES = J // HALF
 TILES = N // P
-CHUNKS = (128, 128, 256, 512)
+CHUNKS = (128, 128, 256, 256, 256)
 WG_CHUNKS = (256, 768)
 
 
@@ -49,20 +49,21 @@ def tile_list_hwayt_gelu_kernel(
                 tab_s[32 * q : 32 * q + 8, :].bitcast(I32),
                 tab_scales[:, 4 * q : 4 * q + 4, :].bitcast(I32),
             )
-        zero_in = keep.tile([P, 1], F32, name="zero_in")
-        nc.vector.memset(zero_in[:], 0.0)
         zero = keep.tile([P, 1], F32, name="zero")
-        nc.scalar.activation(zero[:], zero_in[:], ACT.Gelu_apprx_tanh, bias=zero_in[:])
-        wg_s = keep.tile([P, PASSES, N], U8, name="wg_s", align_bytes=64)
-        nc.vector.memset(wg_s[:].rearrange("p a t -> p (a t)").bitcast(I32), 0)
+        with tc.tile_pool(name="setup", bufs=1) as setup:
+            zero_in = setup.tile([P, 1], F32, name="zero_in")
+            nc.vector.memset(zero_in[:], 0.0)
+            nc.scalar.activation(zero[:], zero_in[:], ACT.Gelu_apprx_tanh, bias=zero_in[:])
+        late = ctx.enter_context(tc.tile_pool(name="late", bufs=1))
         v_s = [keep.tile([P, J], U8, name="v_s%d" % a, align_bytes=64) for a in range(PASSES)]
         nc.vector.memset(v_s[1][:].bitcast(I32), 0)
-
-        bg_rows = keep.tile([P, P], F32, name="bg_rows")
-        nc.gpsimd.memset(bg_rows[:], 0.0)
-        nc.gpsimd.dma_start(bg_rows[0:TILES, :], bg.rearrange("(c p) -> c p", p=P))
         ident = keep.tile([P, P], F32, name="ident")
         make_identity(nc, ident[:])
+
+        bg_rows = late.tile([P, P], F32, name="bg_rows")
+        nc.gpsimd.memset(bg_rows[:], 0.0)
+        wg_s = late.tile([P, PASSES, N], U8, name="wg_s", align_bytes=64)
+        nc.gpsimd.memset(wg_s[:].rearrange("p a t -> p (a t)").bitcast(I32), 0)
 
         wg_starts = [sum(WG_CHUNKS[:c]) for c in range(len(WG_CHUNKS))]
         starts = [sum(CHUNKS[:c]) for c in range(len(CHUNKS))]
@@ -70,34 +71,36 @@ def tile_list_hwayt_gelu_kernel(
 
         def load_wh(c):
             for a in range(PASSES):
-                wh_raw[c, a] = keep.tile([P, PACK, CHUNKS[c]], F32, name="wh_raw%d_%d" % (c, a))
+                wh_raw[c, a] = (late if c else keep).tile([P, PACK, CHUNKS[c]], F32, name="wh_raw%d_%d" % (c, a))
                 rows = wh[512 * a : 512 * (a + 1), starts[c] : starts[c] + CHUNKS[c]]
                 nc.sync.dma_start(wh_raw[c, a][:], rows.rearrange("(p i) n -> p i n", i=PACK))
 
         def load_wg(c):
-            wg_w[c] = keep.tile([P, PASSES, WG_CHUNKS[c]], I32, name="wg_w%d" % c, align_bytes=64)
+            wg_w[c] = late.tile([P, PASSES, WG_CHUNKS[c]], I32, name="wg_w%d" % c, align_bytes=64)
             words = wg_words.rearrange("a p n i -> p a (n i)")
             nc.sync.dma_start(wg_w[c][:], words[:, :, 4 * wg_starts[c] : 4 * (wg_starts[c] + WG_CHUNKS[c])].bitcast(I32))
 
         def load_r(i):
-            r[i] = keep.tile([P, T], F32, name="r%d" % i)
+            r[i] = late.tile([P, T], F32, name="r%d" % i)
             nc.sync.dma_start(r[i][:], rT[P * i : P * (i + 1), :])
 
         load_wh(0)
+        load_r(0)
+        nc.scalar.dma_start(bg_rows[0:TILES, :], bg.rearrange("(c p) -> c p", p=P))
+        load_wg(0)
+        load_wh(1)
         for q in range(4):
             nc.sync.dma_start(
                 wg_s[32 * q : 32 * q + 4, :, :].bitcast(I32),
                 wg_scales[:, 4 * q : 4 * q + 4, :].rearrange("a r n -> r a n").bitcast(I32),
             )
-        load_r(0)
-        load_wg(0)
-        load_wh(1)
-        load_r(1)
         load_wh(2)
-        load_r(2)
+        load_r(1)
         load_wg(1)
-        load_r(3)
         load_wh(3)
+        load_r(2)
+        load_r(3)
+        load_wh(4)
         for i in range(4, TILES):
             load_r(i)
 
@@ -106,13 +109,17 @@ def tile_list_hwayt_gelu_kernel(
         half_bg = keep.tile([P, TILES], F32, name="half_bg")
         nc.scalar.activation(half_bg[:], bg_t[:, 0:TILES], ACT.Copy, scale=0.5)
 
+        def picks(h):
+            return offsets[:, h * (HALF // 16) : (h + 1) * (HALF // 16)]
+
         nc.vector.tensor_copy(v_s[0][:], tab_s[:].indirect(offsets[:]))
         nc.scalar.dma_start(v_s[1][0:100, :].bitcast(I32), v_s[0][4:104, :].bitcast(I32))
+
         v_w = {}
-        for h in range(HALVES):
-            picks = offsets[:, h * (HALF // 16) : (h + 1) * (HALF // 16)]
-            pairs = keep.tile([P, HALF], U32, name="pairs%d" % h, align_bytes=64)
-            nc.vector.tensor_copy(pairs[:], tab_w[:].bitcast(U32).indirect(picks))
+
+        def gather_words(h):
+            pairs = keep.tile([P, HALF], U32, name="pairs%d" % h, tag="stage%d" % h, align_bytes=64)
+            nc.vector.tensor_copy(pairs[:], tab_w[:].bitcast(U32).indirect(picks(h)))
             v_w[h] = keep.tile([P, PASSES, HALF], U16, name="v_w%d" % h, align_bytes=64)
             nc.vector.tensor_copy(v_w[h][:], pairs[:].bitcast(U16).rearrange("p (j a) -> p a j", a=PASSES))
 
@@ -120,7 +127,10 @@ def tile_list_hwayt_gelu_kernel(
 
         def quantize_wh(c):
             for a in range(PASSES):
-                grouped = ring.tile([P, CHUNKS[c], PACK], BF16, name="grouped", tag="grouped", align_bytes=64)
+                if c == 0 and a == PASSES - 1:
+                    grouped = keep.tile([P, CHUNKS[c], PACK], BF16, name="grouped0", tag="stage1", align_bytes=64)
+                else:
+                    grouped = ring.tile([P, CHUNKS[c], PACK], BF16, name="grouped", tag="grouped", align_bytes=64)
                 nc.scalar.copy(
                     grouped[:].rearrange("p (c n) i -> p c i n", n=4),
                     wh_raw[c, a][:].rearrange("p i (c n) -> p c i n", n=4),
@@ -145,10 +155,11 @@ def tile_list_hwayt_gelu_kernel(
                     stop=(a == PASSES - 1),
                 )
 
+        gather_words(0)
+        quantize_wh(0)
+        gather_words(1)
         for i in range(TILES):
             c = max(x for x in range(len(CHUNKS)) if starts[x] <= P * i)
-            if starts[c] == P * i:
-                quantize_wh(c)
             cols = slice(P * i - starts[c], P * (i + 1) - starts[c])
             g = max(x for x in range(len(WG_CHUNKS)) if wg_starts[x] <= P * i)
             gcols = slice(P * i - wg_starts[g], P * (i + 1) - wg_starts[g])
@@ -164,12 +175,13 @@ def tile_list_hwayt_gelu_kernel(
                 ga = psum.tile([P, HALF], F32, name="ga", tag="ga")
                 product(ga, h, [wg_w[g][:, a, gcols] for a in range(PASSES)], [wg_s[:, a, P * i : P * (i + 1)] for a in range(PASSES)])
                 nc.scalar.activation(th[:, js], ga[:], ACT.Tanh, bias=half_bg[:, i : i + 1], scale=0.5)
+            if P * (i + 1) in starts:
+                quantize_wh(c + 1)
             diff = {}
             for h in range(HALVES):
                 js = slice(h * HALF, (h + 1) * HALF)
-                picks = offsets[:, h * (HALF // 16) : (h + 1) * (HALF // 16)]
                 diff[h] = ring.tile([P, HALF], F32, name="diff%d" % h, tag="diff%d" % h)
-                nc.vector.tensor_tensor(diff[h][:], r[i][:].indirect(picks), made[:, js], ALU.subtract)
+                nc.vector.tensor_tensor(diff[h][:], r[i][:].indirect(picks(h)), made[:, js], ALU.subtract)
             for h in range(HALVES):
                 js = slice(h * HALF, (h + 1) * HALF)
                 nc.vector.scalar_tensor_tensor(th[:, js], th[:, js], 1.0, diff[h][:], ALU.subtract, ALU.mult)

@@ -36,27 +36,36 @@ def tile_list_hwayt_gelu_kernel(
         ring = ctx.enter_context(tc.tile_pool(name="ring", bufs=2))
         psum = ctx.enter_context(tc.psum_pool(name="psum", bufs=4))
 
+        def picks(h):
+            return offsets[:, h * (HALF // 16) : (h + 1) * (HALF // 16)]
+
         offsets = keep.tile([P, J // 16], U16, name="offsets")
-        nc.sync.dma_start(offsets[:], offs)
+        picked_s = keep.tile([P, J], U8, name="picked_s", align_bytes=64)
+        with tc.tile_pool(name="setup", bufs=1) as setup:
+            tab_s = setup.tile([P, T], U8, name="tab_s", align_bytes=64)
+            for q in range(4):
+                nc.vector.memset(tab_s[32 * q : 32 * q + 24, :].bitcast(I32), 0)
+                nc.sync.dma_start(
+                    tab_s[32 * q + 24 : 32 * q + 32, :].bitcast(I32),
+                    tab_scales[:, 4 * q : 4 * q + 4, :].bitcast(I32),
+                )
+            nc.sync.dma_start(offsets[:], offs)
+            nc.vector.tensor_copy(picked_s[:], tab_s[:].indirect(offsets[:]))
+        late = ctx.enter_context(tc.tile_pool(name="late", bufs=1))
 
         tab_w = keep.tile([P, T], I32, name="tab_w", align_bytes=64)
         nc.sync.dma_start(tab_w[:], tab_words[0].rearrange("p t i -> p (t i)").bitcast(I32))
 
-        tab_s = keep.tile([P, T], U8, name="tab_s", align_bytes=64)
-        nc.vector.memset(tab_s[:].bitcast(I32), 0)
-        for q in range(4):
-            nc.scalar.dma_start(
-                tab_s[32 * q : 32 * q + 8, :].bitcast(I32),
-                tab_scales[:, 4 * q : 4 * q + 4, :].bitcast(I32),
-            )
-        zero = keep.tile([P, 1], F32, name="zero")
-        with tc.tile_pool(name="setup", bufs=1) as setup:
-            zero_in = setup.tile([P, 1], F32, name="zero_in")
-            nc.vector.memset(zero_in[:], 0.0)
-            nc.scalar.activation(zero[:], zero_in[:], ACT.Gelu_apprx_tanh, bias=zero_in[:])
-        late = ctx.enter_context(tc.tile_pool(name="late", bufs=1))
         v_s = [keep.tile([P, J], U8, name="v_s%d" % a, align_bytes=64) for a in range(PASSES)]
-        nc.vector.memset(v_s[1][:].bitcast(I32), 0)
+        for a in range(PASSES):
+            first = 24 + 4 * a
+            nc.gpsimd.memset(v_s[a][:].bitcast(I32), 0)
+            nc.sync.dma_start(v_s[a][0 : P - first, :].bitcast(I32), picked_s[first:P, :].bitcast(I32))
+
+        zero_in = keep.tile([P, 1], F32, name="zero_in")
+        nc.gpsimd.memset(zero_in[:], 0.0)
+        zero = keep.tile([P, 1], F32, name="zero")
+        nc.scalar.activation(zero[:], zero_in[:], ACT.Gelu_apprx_tanh, bias=zero_in[:])
         ident = keep.tile([P, P], F32, name="ident")
         make_identity(nc, ident[:])
 
@@ -81,39 +90,35 @@ def tile_list_hwayt_gelu_kernel(
             nc.sync.dma_start(wg_w[c][:], words[:, :, 4 * wg_starts[c] : 4 * (wg_starts[c] + WG_CHUNKS[c])].bitcast(I32))
 
         def load_r(i):
-            r[i] = late.tile([P, T], F32, name="r%d" % i)
+            r[i] = (late if i else keep).tile([P, T], F32, name="r%d" % i, tag="slot%d" % i)
             nc.sync.dma_start(r[i][:], rT[P * i : P * (i + 1), :])
 
-        load_wh(0)
         load_r(0)
-        nc.scalar.dma_start(bg_rows[0:TILES, :], bg.rearrange("(c p) -> c p", p=P))
+        load_wh(0)
+        load_r(1)
         load_wg(0)
-        load_wh(1)
+        nc.sync.dma_start(bg_rows[0:TILES, :], bg.rearrange("(c p) -> c p", p=P))
         for q in range(4):
             nc.sync.dma_start(
                 wg_s[32 * q : 32 * q + 4, :, :].bitcast(I32),
                 wg_scales[:, 4 * q : 4 * q + 4, :].rearrange("a r n -> r a n").bitcast(I32),
             )
-        load_wh(2)
-        load_r(1)
-        load_wg(1)
-        load_wh(3)
+        load_wh(1)
         load_r(2)
+        load_wh(2)
+        load_wg(1)
         load_r(3)
+        load_wh(3)
+        load_r(4)
+        load_r(5)
         load_wh(4)
-        for i in range(4, TILES):
-            load_r(i)
+        load_r(6)
+        load_r(7)
 
         bg_t = psum.tile([P, P], F32, name="bg_t", tag="ga")
         nc.tensor.transpose(bg_t[:], bg_rows[:], ident[:])
         half_bg = keep.tile([P, TILES], F32, name="half_bg")
         nc.scalar.activation(half_bg[:], bg_t[:, 0:TILES], ACT.Copy, scale=0.5)
-
-        def picks(h):
-            return offsets[:, h * (HALF // 16) : (h + 1) * (HALF // 16)]
-
-        nc.vector.tensor_copy(v_s[0][:], tab_s[:].indirect(offsets[:]))
-        nc.scalar.dma_start(v_s[1][0:100, :].bitcast(I32), v_s[0][4:104, :].bitcast(I32))
 
         v_w = {}
 
@@ -127,10 +132,7 @@ def tile_list_hwayt_gelu_kernel(
 
         def quantize_wh(c):
             for a in range(PASSES):
-                if c == 0 and a == PASSES - 1:
-                    grouped = keep.tile([P, CHUNKS[c], PACK], BF16, name="grouped0", tag="stage1", align_bytes=64)
-                else:
-                    grouped = ring.tile([P, CHUNKS[c], PACK], BF16, name="grouped", tag="grouped", align_bytes=64)
+                grouped = ring.tile([P, CHUNKS[c], PACK], BF16, name="grouped", tag="grouped", align_bytes=64)
                 nc.scalar.copy(
                     grouped[:].rearrange("p (c n) i -> p c i n", n=4),
                     wh_raw[c, a][:].rearrange("p i (c n) -> p c i n", n=4),
@@ -155,9 +157,20 @@ def tile_list_hwayt_gelu_kernel(
                     stop=(a == PASSES - 1),
                 )
 
+        carried = {}
+
+        def gather_r(i):
+            carried[i] = ring.tile([P, J], F32, name="carried", tag="carried")
+            nc.vector.tensor_copy(carried[i][:], r[i][:].indirect(offsets[:]))
+
+        def slot(i, name):
+            return (late if i else keep).tile([P, J], F32, name=name, tag="slot%d" % i)
+
+        halves = [slice(h * HALF, (h + 1) * HALF) for h in range(HALVES)]
         gather_words(0)
-        quantize_wh(0)
         gather_words(1)
+        gather_r(0)
+        quantize_wh(0)
         for i in range(TILES):
             c = max(x for x in range(len(CHUNKS)) if starts[x] <= P * i)
             cols = slice(P * i - starts[c], P * (i + 1) - starts[c])
@@ -166,31 +179,30 @@ def tile_list_hwayt_gelu_kernel(
             made = keep.tile([P, J], F32, name="made%d" % i)
             th = keep.tile([P, J], F32, name="th%d" % i)
             for h in range(HALVES):
-                js = slice(h * HALF, (h + 1) * HALF)
                 ha = psum.tile([P, HALF], F32, name="ha", tag="ha")
                 product(ha, h, [wh_w[c, a][:, cols] for a in range(PASSES)], [wh_s[c, a][:, cols] for a in range(PASSES)])
-                nc.scalar.activation(made[:, js], ha[:], ACT.Gelu_apprx_tanh, bias=zero[:])
+                nc.scalar.activation(made[:, halves[h]], ha[:], ACT.Gelu_apprx_tanh, bias=zero[:])
             for h in range(HALVES):
-                js = slice(h * HALF, (h + 1) * HALF)
                 ga = psum.tile([P, HALF], F32, name="ga", tag="ga")
                 product(ga, h, [wg_w[g][:, a, gcols] for a in range(PASSES)], [wg_s[:, a, P * i : P * (i + 1)] for a in range(PASSES)])
-                nc.scalar.activation(th[:, js], ga[:], ACT.Tanh, bias=half_bg[:, i : i + 1], scale=0.5)
+                nc.scalar.activation(th[:, halves[h]], ga[:], ACT.Tanh, bias=half_bg[:, i : i + 1], scale=0.5)
             if P * (i + 1) in starts:
                 quantize_wh(c + 1)
-            diff = {}
-            for h in range(HALVES):
-                js = slice(h * HALF, (h + 1) * HALF)
-                diff[h] = ring.tile([P, HALF], F32, name="diff%d" % h, tag="diff%d" % h)
-                nc.vector.tensor_tensor(diff[h][:], r[i][:].indirect(picks(h)), made[:, js], ALU.subtract)
-            for h in range(HALVES):
-                js = slice(h * HALF, (h + 1) * HALF)
-                nc.vector.scalar_tensor_tensor(th[:, js], th[:, js], 1.0, diff[h][:], ALU.subtract, ALU.mult)
-            for h in range(HALVES):
-                js = slice(h * HALF, (h + 1) * HALF)
-                nc.vector.scalar_tensor_tensor(made[:, js], th[:, js], -0.5, made[:, js], ALU.mult, ALU.add)
-            if i < TILES - 1:
+            diff = slot(i, "diff%d" % i)
+            if i + 1 < TILES:
+                nc.gpsimd.tensor_tensor(diff[:], carried[i][:], made[:], ALU.subtract)
+                gather_r(i + 1)
+                gated = slot(i + 1, "gated%d" % i)
+            else:
+                for js in halves:
+                    nc.vector.tensor_tensor(diff[:, js], carried[i][:, js], made[:, js], ALU.subtract)
+                gated = th
+            for js in halves:
+                nc.vector.scalar_tensor_tensor(gated[:, js], th[:, js], 1.0, diff[:, js], ALU.subtract, ALU.mult)
+            for js in halves:
+                nc.vector.scalar_tensor_tensor(made[:, js], gated[:, js], -0.5, made[:, js], ALU.mult, ALU.add)
+            if i + 1 < TILES:
                 nc.sync.dma_start(out[P * i : P * (i + 1), :], made[:])
             else:
-                for h in range(HALVES):
-                    js = slice(h * HALF, (h + 1) * HALF)
+                for js in halves:
                     nc.sync.dma_start(out[P * i : P * (i + 1), js], made[:, js])

@@ -23,8 +23,8 @@ PASSES = K // (P * PACK)
 HALF = 512
 HALVES = J // HALF
 TILES = N // P
-CHUNKS = (128, 128, 256, 256, 256)
-WG_CHUNKS = (256, 768)
+CHUNKS = (128, 128, 128, 128, 256, 256)
+WG_CHUNKS = (256, 256, 512)
 
 
 def tile_list_hwayt_gelu_kernel(
@@ -40,27 +40,25 @@ def tile_list_hwayt_gelu_kernel(
             return offsets[:, h * (HALF // 16) : (h + 1) * (HALF // 16)]
 
         offsets = keep.tile([P, J // 16], U16, name="offsets")
-        picked_s = keep.tile([P, J], U8, name="picked_s", align_bytes=64)
-        with tc.tile_pool(name="setup", bufs=1) as setup:
-            tab_s = setup.tile([P, T], U8, name="tab_s", align_bytes=64)
-            for q in range(4):
-                nc.vector.memset(tab_s[32 * q : 32 * q + 24, :].bitcast(I32), 0)
-                nc.sync.dma_start(
-                    tab_s[32 * q + 24 : 32 * q + 32, :].bitcast(I32),
-                    tab_scales[:, 4 * q : 4 * q + 4, :].bitcast(I32),
-                )
-            nc.sync.dma_start(offsets[:], offs)
-            nc.vector.tensor_copy(picked_s[:], tab_s[:].indirect(offsets[:]))
-        late = ctx.enter_context(tc.tile_pool(name="late", bufs=1))
-
+        nc.sync.dma_start(offsets[:], offs)
+        bg_rows = keep.tile([P, P], F32, name="bg_rows")
+        nc.gpsimd.memset(bg_rows[:], 0.0)
+        nc.sync.dma_start(bg_rows[0:TILES, :], bg.rearrange("(c p) -> c p", p=P))
+        tab_s = keep.tile([P, T], U8, name="tab_s", align_bytes=64)
+        nc.vector.memset(tab_s[:].bitcast(I32), 0)
+        for row in range(4):
+            nc.sync.dma_start(
+                tab_s[row:P:16, :].bitcast(I32),
+                tab_scales[:, row:16:4, :].rearrange("a q t -> q a t").bitcast(I32),
+            )
         tab_w = keep.tile([P, T], I32, name="tab_w", align_bytes=64)
         nc.sync.dma_start(tab_w[:], tab_words[0].rearrange("p t i -> p (t i)").bitcast(I32))
 
         v_s = [keep.tile([P, J], U8, name="v_s%d" % a, align_bytes=64) for a in range(PASSES)]
-        for a in range(PASSES):
-            first = 24 + 4 * a
-            nc.gpsimd.memset(v_s[a][:].bitcast(I32), 0)
-            nc.sync.dma_start(v_s[a][0 : P - first, :].bitcast(I32), picked_s[first:P, :].bitcast(I32))
+        nc.vector.memset(v_s[1][:].bitcast(I32), 0)
+        wg_s = keep.tile([P, PASSES, N], U8, name="wg_s", align_bytes=64)
+        nc.vector.memset(wg_s[:].rearrange("p a t -> p (a t)").bitcast(I32), 0)
+        nc.vector.tensor_copy(v_s[0][:], tab_s[:].indirect(offsets[:]))
 
         zero_in = keep.tile([P, 1], F32, name="zero_in")
         nc.gpsimd.memset(zero_in[:], 0.0)
@@ -69,49 +67,46 @@ def tile_list_hwayt_gelu_kernel(
         ident = keep.tile([P, P], F32, name="ident")
         make_identity(nc, ident[:])
 
-        bg_rows = late.tile([P, P], F32, name="bg_rows")
-        nc.gpsimd.memset(bg_rows[:], 0.0)
-        wg_s = late.tile([P, PASSES, N], U8, name="wg_s", align_bytes=64)
-        nc.gpsimd.memset(wg_s[:].rearrange("p a t -> p (a t)").bitcast(I32), 0)
-
         wg_starts = [sum(WG_CHUNKS[:c]) for c in range(len(WG_CHUNKS))]
         starts = [sum(CHUNKS[:c]) for c in range(len(CHUNKS))]
         wh_raw, wg_w, r = {}, {}, {}
 
         def load_wh(c):
             for a in range(PASSES):
-                wh_raw[c, a] = (late if c else keep).tile([P, PACK, CHUNKS[c]], F32, name="wh_raw%d_%d" % (c, a))
+                wh_raw[c, a] = keep.tile([P, PACK, CHUNKS[c]], F32, name="wh_raw%d_%d" % (c, a))
                 rows = wh[512 * a : 512 * (a + 1), starts[c] : starts[c] + CHUNKS[c]]
                 nc.sync.dma_start(wh_raw[c, a][:], rows.rearrange("(p i) n -> p i n", i=PACK))
 
         def load_wg(c):
-            wg_w[c] = late.tile([P, PASSES, WG_CHUNKS[c]], I32, name="wg_w%d" % c, align_bytes=64)
+            wg_w[c] = keep.tile([P, PASSES, WG_CHUNKS[c]], I32, name="wg_w%d" % c, align_bytes=64)
             words = wg_words.rearrange("a p n i -> p a (n i)")
             nc.sync.dma_start(wg_w[c][:], words[:, :, 4 * wg_starts[c] : 4 * (wg_starts[c] + WG_CHUNKS[c])].bitcast(I32))
 
         def load_r(i):
-            r[i] = (late if i else keep).tile([P, T], F32, name="r%d" % i, tag="slot%d" % i)
+            r[i] = keep.tile([P, T], F32, name="r%d" % i, tag="slot%d" % i)
             nc.sync.dma_start(r[i][:], rT[P * i : P * (i + 1), :])
 
-        load_r(0)
         load_wh(0)
-        load_r(1)
+        load_r(0)
+        nc.sync.dma_start(v_s[1][0:112, :].bitcast(I32), v_s[0][16:P, :].bitcast(I32))
         load_wg(0)
-        nc.sync.dma_start(bg_rows[0:TILES, :], bg.rearrange("(c p) -> c p", p=P))
         for q in range(4):
             nc.sync.dma_start(
                 wg_s[32 * q : 32 * q + 4, :, :].bitcast(I32),
                 wg_scales[:, 4 * q : 4 * q + 4, :].rearrange("a r n -> r a n").bitcast(I32),
             )
         load_wh(1)
-        load_r(2)
         load_wh(2)
-        load_wg(1)
-        load_r(3)
+        load_r(1)
         load_wh(3)
-        load_r(4)
-        load_r(5)
+        load_wg(1)
+        load_r(2)
         load_wh(4)
+        load_r(3)
+        load_wg(2)
+        load_r(4)
+        load_wh(5)
+        load_r(5)
         load_r(6)
         load_r(7)
 
@@ -134,8 +129,8 @@ def tile_list_hwayt_gelu_kernel(
             for a in range(PASSES):
                 grouped = ring.tile([P, CHUNKS[c], PACK], BF16, name="grouped", tag="grouped", align_bytes=64)
                 nc.scalar.copy(
-                    grouped[:].rearrange("p (c n) i -> p c i n", n=4),
-                    wh_raw[c, a][:].rearrange("p i (c n) -> p c i n", n=4),
+                    grouped[:],
+                    wh_raw[c, a][:].rearrange("p i n -> p n i"),
                 )
                 wh_w[c, a] = keep.tile([P, CHUNKS[c]], U32, name="wh_w%d_%d" % (c, a), align_bytes=64)
                 wh_s[c, a] = keep.tile([P, CHUNKS[c]], U8, name="wh_s%d_%d" % (c, a), align_bytes=64)
@@ -157,52 +152,60 @@ def tile_list_hwayt_gelu_kernel(
                     stop=(a == PASSES - 1),
                 )
 
-        carried = {}
-
-        def gather_r(i):
-            carried[i] = ring.tile([P, J], F32, name="carried", tag="carried")
-            nc.vector.tensor_copy(carried[i][:], r[i][:].indirect(offsets[:]))
-
-        def slot(i, name):
-            return (late if i else keep).tile([P, J], F32, name=name, tag="slot%d" % i)
-
         halves = [slice(h * HALF, (h + 1) * HALF) for h in range(HALVES)]
-        gather_words(0)
-        gather_words(1)
-        gather_r(0)
-        quantize_wh(0)
-        for i in range(TILES):
+        made, th, diff = {}, {}, {}
+
+        def activations(i):
             c = max(x for x in range(len(CHUNKS)) if starts[x] <= P * i)
+            if starts[c] == P * i:
+                quantize_wh(c)
             cols = slice(P * i - starts[c], P * (i + 1) - starts[c])
             g = max(x for x in range(len(WG_CHUNKS)) if wg_starts[x] <= P * i)
             gcols = slice(P * i - wg_starts[g], P * (i + 1) - wg_starts[g])
-            made = keep.tile([P, J], F32, name="made%d" % i)
-            th = keep.tile([P, J], F32, name="th%d" % i)
+            made[i] = keep.tile([P, J], F32, name="made%d" % i)
+            th[i] = keep.tile([P, J], F32, name="th%d" % i)
             for h in range(HALVES):
                 ha = psum.tile([P, HALF], F32, name="ha", tag="ha")
                 product(ha, h, [wh_w[c, a][:, cols] for a in range(PASSES)], [wh_s[c, a][:, cols] for a in range(PASSES)])
-                nc.scalar.activation(made[:, halves[h]], ha[:], ACT.Gelu_apprx_tanh, bias=zero[:])
+                nc.scalar.activation(made[i][:, halves[h]], ha[:], ACT.Gelu_apprx_tanh, bias=zero[:])
             for h in range(HALVES):
                 ga = psum.tile([P, HALF], F32, name="ga", tag="ga")
                 product(ga, h, [wg_w[g][:, a, gcols] for a in range(PASSES)], [wg_s[:, a, P * i : P * (i + 1)] for a in range(PASSES)])
-                nc.scalar.activation(th[:, halves[h]], ga[:], ACT.Tanh, bias=half_bg[:, i : i + 1], scale=0.5)
-            if P * (i + 1) in starts:
-                quantize_wh(c + 1)
-            diff = slot(i, "diff%d" % i)
-            if i + 1 < TILES:
-                nc.gpsimd.tensor_tensor(diff[:], carried[i][:], made[:], ALU.subtract)
-                gather_r(i + 1)
-                gated = slot(i + 1, "gated%d" % i)
-            else:
-                for js in halves:
-                    nc.vector.tensor_tensor(diff[:, js], carried[i][:, js], made[:, js], ALU.subtract)
-                gated = th
-            for js in halves:
-                nc.vector.scalar_tensor_tensor(gated[:, js], th[:, js], 1.0, diff[:, js], ALU.subtract, ALU.mult)
-            for js in halves:
-                nc.vector.scalar_tensor_tensor(made[:, js], gated[:, js], -0.5, made[:, js], ALU.mult, ALU.add)
-            if i + 1 < TILES:
-                nc.sync.dma_start(out[P * i : P * (i + 1), :], made[:])
-            else:
-                for js in halves:
-                    nc.sync.dma_start(out[P * i : P * (i + 1), js], made[:, js])
+                nc.scalar.activation(th[i][:, halves[h]], ga[:], ACT.Tanh, bias=half_bg[:, i : i + 1], scale=0.5)
+
+        def difference(i):
+            diff[i] = ring.tile([P, J], F32, name="diff", tag="diff")
+            nc.vector.tensor_tensor(diff[i][:], r[i][:].indirect(offsets[:]), made[i][:], ALU.subtract)
+
+        def gate(i, js):
+            nc.vector.scalar_tensor_tensor(th[i][:, js], th[i][:, js], 1.0, diff[i][:, js], ALU.subtract, ALU.mult)
+
+        def finish(i, result, js):
+            nc.vector.scalar_tensor_tensor(result[:, js], th[i][:, js], -0.5, made[i][:, js], ALU.mult, ALU.add)
+            nc.sync.dma_start(out[P * i : P * (i + 1), js], result[:, js])
+
+        gather_words(0)
+        gather_words(1)
+        activations(0)
+        carried = keep.tile([P, J], F32, name="carried")
+        nc.vector.tensor_copy(carried[:], r[0][:].indirect(offsets[:]))
+        activations(1)
+        diff[0] = ring.tile([P, J], F32, name="diff", tag="diff")
+        for js in halves:
+            nc.vector.tensor_tensor(diff[0][:, js], carried[:, js], made[0][:, js], ALU.subtract)
+        for js in halves:
+            gate(0, js)
+        whole = slice(0, J)
+        for i in range(TILES - 1):
+            if i + 2 < TILES:
+                activations(i + 2)
+            difference(i + 1)
+            result = keep.tile([P, J], F32, name="result%d" % i, tag="slot%d" % (i + 1))
+            finish(i, result, whole)
+            if i + 2 < TILES:
+                gate(i + 1, whole)
+        last = TILES - 1
+        for js in halves:
+            gate(last, js)
+        for js in halves:
+            finish(last, made[last], js)

from contextlib import ExitStack

import concourse.mybir as mybir
from concourse.masks import make_identity

K, N, T, J = 1024, 1024, 2048, 1024
FLOPS = 2 * 2 * K * N * J

F32 = mybir.dt.float32
BF16 = mybir.dt.bfloat16
I32 = mybir.dt.int32
U32 = mybir.dt.uint32
U16 = mybir.dt.uint16
U8 = mybir.dt.uint8
FP8X4 = mybir.dt.float8_e4m3fn_x4
FP4X4 = mybir.dt.float4_e2m1fn_x4
ALU = mybir.AluOpType
ACT = mybir.ActivationFunctionType

P = 128
PACK = 4
PASSES = K // (P * PACK)
HALF = 512
HALVES = J // HALF
TILES = N // P
CHUNKS = (128, 128, 128, 128, 256, 256)
WG_CHUNKS = (256, 256, 512)


def tile_list_hwayt_gelu_kernel(
    tc, tab_words, tab_scales, wg_words, wg_scales, wh, bg, rT, offs, out
):
    nc = tc.nc
    with ExitStack() as ctx:
        keep = ctx.enter_context(tc.tile_pool(name="keep", bufs=1))
        ring = ctx.enter_context(tc.tile_pool(name="ring", bufs=2))
        psum = ctx.enter_context(tc.psum_pool(name="psum", bufs=4))

        def picks(h):
            return offsets[:, h * (HALF // 16) : (h + 1) * (HALF // 16)]

        offsets = keep.tile([P, J // 16], U16, name="offsets")
        nc.sync.dma_start(offsets[:], offs)
        bg_rows = keep.tile([P, P], F32, name="bg_rows")
        nc.gpsimd.memset(bg_rows[:], 0.0)
        nc.sync.dma_start(bg_rows[0:TILES, :], bg.rearrange("(c p) -> c p", p=P))
        tab_s = keep.tile([P, T], U8, name="tab_s", align_bytes=64)
        nc.vector.memset(tab_s[:].bitcast(I32), 0)
        for row in range(4):
            nc.sync.dma_start(
                tab_s[row:P:16, :].bitcast(I32),
                tab_scales[:, row:16:4, :].rearrange("a q t -> q a t").bitcast(I32),
            )
        tab_w = keep.tile([P, T], I32, name="tab_w", align_bytes=64)
        nc.sync.dma_start(tab_w[:], tab_words[0].rearrange("p t i -> p (t i)").bitcast(I32))

        v_s = [keep.tile([P, J], U8, name="v_s%d" % a, align_bytes=64) for a in range(PASSES)]
        nc.vector.memset(v_s[1][:].bitcast(I32), 0)
        wg_s = keep.tile([P, PASSES, N], U8, name="wg_s", align_bytes=64)
        nc.vector.memset(wg_s[:].rearrange("p a t -> p (a t)").bitcast(I32), 0)
        nc.vector.tensor_copy(v_s[0][:], tab_s[:].indirect(offsets[:]))

        zero_in = keep.tile([P, 1], F32, name="zero_in")
        nc.gpsimd.memset(zero_in[:], 0.0)
        zero = keep.tile([P, 1], F32, name="zero")
        nc.scalar.activation(zero[:], zero_in[:], ACT.Gelu_apprx_tanh, bias=zero_in[:])
        ident = keep.tile([P, P], F32, name="ident")
        make_identity(nc, ident[:])

        wg_starts = [sum(WG_CHUNKS[:c]) for c in range(len(WG_CHUNKS))]
        starts = [sum(CHUNKS[:c]) for c in range(len(CHUNKS))]
        wh_raw, wg_w, r = {}, {}, {}

        def load_wh(c):
            for a in range(PASSES):
                wh_raw[c, a] = keep.tile([P, PACK, CHUNKS[c]], F32, name="wh_raw%d_%d" % (c, a))
                rows = wh[512 * a : 512 * (a + 1), starts[c] : starts[c] + CHUNKS[c]]
                nc.sync.dma_start(wh_raw[c, a][:], rows.rearrange("(p i) n -> p i n", i=PACK))

        def load_wg(c):
            wg_w[c] = keep.tile([P, PASSES, WG_CHUNKS[c]], I32, name="wg_w%d" % c, align_bytes=64)
            words = wg_words.rearrange("a p n i -> p a (n i)")
            nc.sync.dma_start(wg_w[c][:], words[:, :, 4 * wg_starts[c] : 4 * (wg_starts[c] + WG_CHUNKS[c])].bitcast(I32))

        def load_r(i):
            r[i] = keep.tile([P, T], F32, name="r%d" % i, tag="slot%d" % i)
            nc.sync.dma_start(r[i][:], rT[P * i : P * (i + 1), :])

        load_wh(0)
        load_r(0)
        nc.sync.dma_start(v_s[1][0:112, :].bitcast(I32), v_s[0][16:P, :].bitcast(I32))
        load_wg(0)
        for q in range(4):
            nc.sync.dma_start(
                wg_s[32 * q : 32 * q + 4, :, :].bitcast(I32),
                wg_scales[:, 4 * q : 4 * q + 4, :].rearrange("a r n -> r a n").bitcast(I32),
            )
        load_wh(1)
        load_wh(2)
        load_r(1)
        load_wh(3)
        load_wg(1)
        load_r(2)
        load_wh(4)
        load_r(3)
        load_wg(2)
        load_r(4)
        load_wh(5)
        load_r(5)
        load_r(6)
        load_r(7)

        bg_t = psum.tile([P, P], F32, name="bg_t", tag="ga")
        nc.tensor.transpose(bg_t[:], bg_rows[:], ident[:])
        half_bg = keep.tile([P, TILES], F32, name="half_bg")
        nc.scalar.activation(half_bg[:], bg_t[:, 0:TILES], ACT.Copy, scale=0.5)

        v_w = {}

        def gather_words(h):
            pairs = keep.tile([P, HALF], U32, name="pairs%d" % h, tag="stage%d" % h, align_bytes=64)
            nc.vector.tensor_copy(pairs[:], tab_w[:].bitcast(U32).indirect(picks(h)))
            v_w[h] = keep.tile([P, PASSES, HALF], U16, name="v_w%d" % h, align_bytes=64)
            nc.vector.tensor_copy(v_w[h][:], pairs[:].bitcast(U16).rearrange("p (j a) -> p a j", a=PASSES))

        wh_w, wh_s = {}, {}

        def quantize_wh(c):
            for a in range(PASSES):
                grouped = ring.tile([P, CHUNKS[c], PACK], BF16, name="grouped", tag="grouped", align_bytes=64)
                nc.scalar.copy(
                    grouped[:],
                    wh_raw[c, a][:].rearrange("p i n -> p n i"),
                )
                wh_w[c, a] = keep.tile([P, CHUNKS[c]], U32, name="wh_w%d_%d" % (c, a), align_bytes=64)
                wh_s[c, a] = keep.tile([P, CHUNKS[c]], U8, name="wh_s%d_%d" % (c, a), align_bytes=64)
                nc.vector.quantize_mx(
                    out=wh_w[c, a][:].bitcast(FP8X4),
                    scales=wh_s[c, a][:],
                    in_=grouped[:].rearrange("p n i -> p (n i)"),
                )

        def product(bank, h, words, scales):
            for a in range(PASSES):
                nc.tensor.matmul_mx(
                    out=bank[:],
                    lhsT=words[a].bitcast(FP8X4),
                    lhsT_scale=scales[a],
                    rhs=v_w[h][:, a, :].bitcast(FP4X4),
                    rhs_scale=v_s[a][:, h * HALF : (h + 1) * HALF],
                    start=(a == 0),
                    stop=(a == PASSES - 1),
                )

        halves = [slice(h * HALF, (h + 1) * HALF) for h in range(HALVES)]
        made, th, diff = {}, {}, {}

        def activations(i):
            c = max(x for x in range(len(CHUNKS)) if starts[x] <= P * i)
            if starts[c] == P * i:
                quantize_wh(c)
            cols = slice(P * i - starts[c], P * (i + 1) - starts[c])
            g = max(x for x in range(len(WG_CHUNKS)) if wg_starts[x] <= P * i)
            gcols = slice(P * i - wg_starts[g], P * (i + 1) - wg_starts[g])
            made[i] = keep.tile([P, J], F32, name="made%d" % i)
            th[i] = keep.tile([P, J], F32, name="th%d" % i)
            for h in range(HALVES):
                ha = psum.tile([P, HALF], F32, name="ha", tag="ha")
                product(ha, h, [wh_w[c, a][:, cols] for a in range(PASSES)], [wh_s[c, a][:, cols] for a in range(PASSES)])
                nc.scalar.activation(made[i][:, halves[h]], ha[:], ACT.Gelu_apprx_tanh, bias=zero[:])
            for h in range(HALVES):
                ga = psum.tile([P, HALF], F32, name="ga", tag="ga")
                product(ga, h, [wg_w[g][:, a, gcols] for a in range(PASSES)], [wg_s[:, a, P * i : P * (i + 1)] for a in range(PASSES)])
                nc.scalar.activation(th[i][:, halves[h]], ga[:], ACT.Tanh, bias=half_bg[:, i : i + 1], scale=0.5)

        def difference(i):
            diff[i] = ring.tile([P, J], F32, name="diff", tag="diff")
            nc.vector.tensor_tensor(diff[i][:], r[i][:].indirect(offsets[:]), made[i][:], ALU.subtract)

        def gate(i, js):
            nc.vector.scalar_tensor_tensor(th[i][:, js], th[i][:, js], 1.0, diff[i][:, js], ALU.subtract, ALU.mult)

        def finish(i, result, js):
            nc.vector.scalar_tensor_tensor(result[:, js], th[i][:, js], -0.5, made[i][:, js], ALU.mult, ALU.add)
            nc.sync.dma_start(out[P * i : P * (i + 1), js], result[:, js])

        gather_words(0)
        gather_words(1)
        activations(0)
        carried = keep.tile([P, J], F32, name="carried")
        nc.vector.tensor_copy(carried[:], r[0][:].indirect(offsets[:]))
        activations(1)
        diff[0] = ring.tile([P, J], F32, name="diff", tag="diff")
        for js in halves:
            nc.vector.tensor_tensor(diff[0][:, js], carried[:, js], made[0][:, js], ALU.subtract)
        for js in halves:
            gate(0, js)
        whole = slice(0, J)
        for i in range(TILES - 1):
            if i + 2 < TILES:
                activations(i + 2)
            difference(i + 1)
            result = keep.tile([P, J], F32, name="result%d" % i, tag="slot%d" % (i + 1))
            finish(i, result, whole)
            if i + 2 < TILES:
                gate(i + 1, whole)
        last = TILES - 1
        for js in halves:
            gate(last, js)
        for js in halves:
            finish(last, made[last], js)
